import numpy as np
import ml_dtypes


def mxq(x, axis, fmt="e4m3"):
    dtype, down = {"e4m3": (ml_dtypes.float8_e4m3fn, 7), "e5m2": (ml_dtypes.float8_e5m2, 14)}[fmt]
    v = np.moveaxis(np.asarray(x, np.float32).astype(ml_dtypes.bfloat16).astype(np.float64), axis, -1)
    blocks = v.reshape(v.shape[:-1] + (-1, 32))
    amax = np.abs(blocks).max(-1, keepdims=True)
    byte = np.maximum(np.where(amax > 0, np.frexp(amax)[1] - 1 + 127, 0) - down, 1)
    scale = np.exp2(byte - 127.0)
    codes = (blocks / scale).astype(np.float32).astype(dtype).astype(np.float64)
    return np.moveaxis((codes * scale).reshape(v.shape), -1, axis)


WIDE = False


def mx_kscale(k):
    if not WIDE:
        return np.ones(k)
    levels = np.array([10, -10, 5, -5, 0])
    if k % 512:
        return np.exp2(np.random.permutation(np.resize(levels, k // 32))).repeat(32)
    a = np.empty((k // 512, 16))
    for p in range(k // 512):
        a[p, :8] = np.random.permutation(np.resize(levels, 8))
        for g in range(8):
            far = levels[np.abs(levels - a[p, g]) >= 10]
            a[p, g + 8] = far[np.random.randint(len(far))]
    return np.exp2(a.ravel()).repeat(32)


BF16 = ml_dtypes.bfloat16


def bf(x):
    return np.asarray(x, np.float32).astype(BF16)


def f64(x):
    return np.asarray(x).astype(np.float64)


E2M1 = np.array([0.0, 0.5, 1.0, 1.5, 2.0, 3.0, 4.0, 6.0, -0.0, -0.5, -1.0, -1.5, -2.0, -3.0, -4.0, -6.0])


def pack_weight(w, fmt):
    k, n = w.shape
    w = f64(bf(w)).reshape(k // 32, 32, n)
    amax = np.abs(w).max(1)
    if fmt == "e4m3":
        byte = np.frexp(amax)[1] - 1 + 127 - 7
    else:
        mant, ex = np.frexp(amax / 6.0)
        byte = np.where(mant > 0.5, ex, ex - 1) + 127
    byte = np.clip(np.where(amax > 0, byte, 1), 1, 254)
    scaled = (w * np.exp2(127.0 - byte)[:, None, :]).reshape(k, n).astype(np.float32)
    by_word = np.ascontiguousarray(scaled.reshape(k // 512, 128, 4, n).transpose(0, 1, 3, 2))
    if fmt == "e4m3":
        words = by_word.astype(ml_dtypes.float8_e4m3fn).view(np.uint8)
    else:
        c = by_word.astype(ml_dtypes.float4_e2m1fn).view(np.uint8) & 0xF
        words = c[..., 0::2] | (c[..., 1::2] << 4)
    return np.ascontiguousarray(words), np.ascontiguousarray(byte.astype(np.uint8).reshape(k // 512, 16, n))


def unpack_weight(words, scales, fmt):
    g, p, n, _ = words.shape
    if fmt == "e4m3":
        vals = np.ascontiguousarray(words).view(ml_dtypes.float8_e4m3fn).astype(np.float64)
    else:
        nib = np.empty((g, p, n, 4), np.uint8)
        nib[..., 0::2] = words & 0xF
        nib[..., 1::2] = words >> 4
        vals = E2M1[nib]
    vals = vals * np.repeat(np.exp2(scales.astype(np.float64) - 127.0), 8, axis=1)[..., None]
    return vals.transpose(0, 1, 3, 2).reshape(g * 512, n)
def pack4(w):
    words, scales = pack_weight(w, "e2m1")
    return words.reshape(words.shape[0], 128, -1), scales


def unpack4(words, scales):
    return unpack_weight(words.reshape(words.shape[0], 128, -1, 2), scales, "e2m1")


def planes(Y):
    n, m = Y.shape
    b = f64(bf(Y)).reshape(n // 32, 32, m)
    amax = np.abs(b).max(1)
    byte = np.clip(np.where(amax > 0, np.frexp(amax)[1] - 1 + 127 - 7, 1), 1, 254)
    codes = (b * np.exp2(127.0 - byte)[:, None, :]).reshape(n, m).astype(np.float32).astype(ml_dtypes.float8_e4m3fn).view(np.uint8)
    words = codes.reshape(n // 512, 128, 4, m).transpose(0, 1, 3, 2)
    return np.ascontiguousarray(words), np.ascontiguousarray(byte.astype(np.uint8).reshape(n // 512, 16, m))


M, K, F, N = 1024, 1536, 1024, 2048


def setup_inputs():
    s = mx_kscale(K)
    t = mx_kscale(F)
    V = np.random.randn(K, F) ** 2 / np.sqrt(3 * K) * s[:, None] * t[None, :]
    R = np.random.randn(F, N) / np.sqrt(F) / t[:, None]
    arrivals = bf(np.random.randn(M, K) / s[None, :])
    visit_words, visit_scales = pack4(V)
    response_words, response_scales = pack4(R)
    return {
        "arrivals": arrivals,
        "visit_words": visit_words,
        "visit_scales": visit_scales,
        "walk_in": bf(0.3 * np.random.randn(F) * t),
        "service": bf(np.exp(0.3 * np.random.randn(F))),
        "response_words": response_words,
        "response_scales": response_scales,
        "standing": bf(0.3 * np.random.randn(N)),
        "recover": bf(0.3 + 0.4 * np.random.rand(N)),
        "wage": bf(np.exp(0.8 * np.random.randn(N))),
    }

def reference(arrivals, visit_words, visit_scales, walk_in, service, response_words, response_scales, standing, recover, wage):
    V = unpack4(visit_words, visit_scales)
    R = unpack4(response_words, response_scales)
    flow = mxq(f64(arrivals), 1, "e4m3") @ V
    load = (flow + f64(walk_in)) / f64(service)
    hours = (mxq(load, 1, "e4m3") @ R) + f64(standing)
    y = np.maximum(hours, f64(recover) * hours) * f64(wage)
    Y = y.T
    words, scales = planes(Y)
    return y, words, scales

@@ -1,0 +1,355 @@
+from contextlib import ExitStack
+
+import concourse.mybir as mybir
+from concourse.masks import make_identity
+
+M, K, F, N = 1024, 1536, 1024, 2048
+FLOPS = 2 * M * K * F + 2 * M * F * N
+
+F32 = mybir.dt.float32
+BF16 = mybir.dt.bfloat16
+I32 = mybir.dt.int32
+U32 = mybir.dt.uint32
+U8 = mybir.dt.uint8
+FP8X4 = mybir.dt.float8_e4m3fn_x4
+FP4X4 = mybir.dt.float4_e2m1fn_x4
+ALU = mybir.AluOpType
+ACT = mybir.ActivationFunctionType
+
+P = 128
+PACK = 4
+GROUP = P * PACK
+HALF = 512
+K_GROUPS = K // GROUP
+F_GROUPS = F // GROUP
+N_GROUPS = N // GROUP
+HALVES = M // HALF
+LINE = 16
+
+
+def tile_staffing_wage_swing_h1_kernel(
+    tc, arrivals, visit_words, visit_scales, walk_in, service, response_words, response_scales,
+    standing, recover, wage, out_0, out_1, out_2,
+):
+    nc = tc.nc
+    with ExitStack() as ctx:
+        keep = ctx.enter_context(tc.tile_pool(name="keep", bufs=1))
+        work = ctx.enter_context(tc.tile_pool(name="work", bufs=2))
+        psum = ctx.enter_context(tc.psum_pool(name="psum", bufs=1))
+        ctx.enter_context(tc.manual_schedule())
+
+        def kept(name, shape, dtype):
+            return keep.tile(shape, dtype, name=name, align_bytes=64)
+
+        banks_taken = []
+
+        def next_bank(shape):
+            name = "bank%d" % (len(banks_taken) % 8)
+            banks_taken.append(name)
+            return psum.tile(shape, F32, name=name, tag=name)
+
+        ident = kept("ident", [P, P], F32)
+        make_identity(nc, ident[:])
+        warm_in = kept("warm_in", [P, 1], F32)
+        warm_out = kept("warm_out", [P, 1], F32)
+        v_scale_raw = kept("v_scale_raw", [P, K_GROUPS, F], U8)
+        r_scale_raw = kept("r_scale_raw", [P, F_GROUPS, N], U8)
+        nc.vector.memset(v_scale_raw[:].rearrange("p g n -> p (g n)").bitcast(I32), 0)
+        nc.vector.memset(warm_in[:], 0.0)
+        nc.vector.memset(r_scale_raw[:].rearrange("p g n -> p (g n)").bitcast(I32), 0)
+        nc.scalar.activation(out=warm_out[:], in_=warm_in[:], func=ACT.Identity)
+
+        v_raw = [kept("v_raw%d" % g, [P, 2 * F], U8) for g in range(K_GROUPS)]
+        r_raw = [kept("r_raw%d" % G, [P, F_GROUPS, 2 * GROUP], U8) for G in range(N_GROUPS)]
+        a_raw = {(h, g): kept("a_raw%d_%d" % (h, g), [P, HALF // P, GROUP], BF16) for h in range(HALVES) for g in range(K_GROUPS)}
+
+        def load_v(g):
+            nc.sync.dma_start(out=v_raw[g][:].bitcast(I32), in_=visit_words[g].bitcast(I32))
+
+        def load_r(G):
+            src = response_words[:, :, 2 * GROUP * G : 2 * GROUP * (G + 1)].rearrange("g p b -> p g b")
+            nc.sync.dma_start(out=r_raw[G][:].bitcast(I32), in_=src.bitcast(I32))
+
+        def load_a(h, g):
+            src = arrivals[HALF * h : HALF * (h + 1), GROUP * g : GROUP * (g + 1)]
+            nc.sync.dma_start(out=a_raw[h, g][:], in_=src.rearrange("(i p) k -> p i k", p=P))
+
+        def load_scales(raw, dram):
+            for quad in range(4):
+                src = dram[:, 4 * quad : 4 * quad + 4, :].rearrange("g r n -> r g n")
+                nc.sync.dma_start(out=raw[32 * quad : 32 * quad + 4].bitcast(I32), in_=src.bitcast(I32))
+
+        def load_vec(name, vec, groups):
+            t = kept(name, [P, groups, PACK], BF16)
+            nc.sync.dma_start(out=t[:], in_=vec.rearrange("(g p t) -> p g t", p=P, t=PACK))
+            return t
+
+        load_v(0)
+        load_a(0, 0)
+        load_scales(v_scale_raw, visit_scales)
+        load_v(1)
+        load_a(0, 1)
+        load_v(2)
+        load_a(0, 2)
+        walk_sb = load_vec("walk_sb", walk_in, F_GROUPS)
+        service_sb = load_vec("service_sb", service, F_GROUPS)
+        load_r(0)
+        load_scales(r_scale_raw, response_scales)
+        load_r(1)
+        load_a(1, 0)
+        load_a(1, 1)
+        load_a(1, 2)
+        standing_sb = load_vec("standing_sb", standing, N_GROUPS)
+        recover_sb = load_vec("recover_sb", recover, N_GROUPS)
+        wage_sb = load_vec("wage_sb", wage, N_GROUPS)
+        load_r(2)
+        load_r(3)
+
+        v_codes = [kept("v_codes%d" % g, [P, PACK, F // 2], U8) for g in range(K_GROUPS)]
+        v_scales = kept("v_scales", [P, PACK, K_GROUPS * F // PACK], U8)
+        r_codes = [kept("r_codes%d" % G, [P, PACK, F_GROUPS * 2 * P], U8) for G in range(N_GROUPS)]
+        r_scales = [kept("r_scales%d" % G, [P, PACK, F_GROUPS * P], U8) for G in range(N_GROUPS)]
+
+        def sort_words(dst, src):
+            nc.vector.tensor_copy(
+                out=dst.rearrange("p t (c i b) -> p c t i b", i=LINE // 2, b=2),
+                in_=src.rearrange("p (c i t b) -> p c t i b", i=LINE // 2, t=PACK, b=2),
+            )
+
+        def sort_v(g):
+            sort_words(v_codes[g][:], v_raw[g][:])
+
+        def sort_r(G):
+            sort_words(r_codes[G][:], r_raw[G][:].rearrange("p g b -> p (g b)"))
+
+        def sort_v_scales():
+            nc.vector.tensor_copy(
+                out=v_scales[:].rearrange("p t (c i) -> p c t i", i=LINE),
+                in_=v_scale_raw[:].rearrange("p g (c i t) -> p (g c) t i", i=LINE, t=PACK),
+            )
+
+        def sort_r_scales(G):
+            nc.vector.tensor_copy(
+                out=r_scales[G][:].rearrange("p t (g c i) -> p g c t i", g=F_GROUPS, i=LINE),
+                in_=r_scale_raw[:, :, GROUP * G : GROUP * (G + 1)].rearrange("p g (c i t) -> p g c t i", i=LINE, t=PACK),
+            )
+
+        inv_service = kept("inv_service", [P, F_GROUPS, PACK], F32)
+        walk_load = kept("walk_load", [P, F_GROUPS, PACK], F32)
+        wage32 = kept("wage32", [P, N_GROUPS, PACK], F32)
+        recover32 = kept("recover32", [P, N_GROUPS, PACK], F32)
+        standing_pay = kept("standing_pay", [P, N_GROUPS, PACK], F32)
+
+        a_codes = {}
+        a_scales = {}
+        a_grouped = {}
+
+        def turn_arrivals(h, g):
+            a_grouped[h, g] = work.tile([P, HALF * PACK], BF16, name="a_grouped", tag="a_grouped", bufs=3, align_bytes=64)
+            words = a_raw[h, g][:].bitcast(F32)
+            for pair in range(2):
+                bank = next_bank([P, 2, 2 * P])
+                for i in range(2):
+                    for u in range(2):
+                        nc.tensor.transpose(bank[:, u, P * i : P * (i + 1)], words[:, 2 * pair + i, u : 2 * P : 2], ident[:])
+                dst = a_grouped[h, g][:].bitcast(F32)[:, 512 * pair : 512 * (pair + 1)]
+                nc.scalar.copy(out=dst.rearrange("p (r u) -> p r u", u=2), in_=bank[:].rearrange("p u r -> p r u"))
+
+        def quantize(codes, scales, grouped):
+            nc.vector.quantize_mx(out=codes.bitcast(FP8X4), scales=scales, in_=grouped)
+
+        def quantize_arrivals(h, g):
+            a_codes[h, g] = kept("a_codes%d_%d" % (h, g), [P, HALF], U32)
+            a_scales[h, g] = kept("a_scales%d_%d" % (h, g), [P, HALF], U8)
+            quantize(a_codes[h, g][:], a_scales[h, g][:], a_grouped[h, g][:])
+
+        def interleave(dst, src, copy=nc.vector.tensor_copy):
+            copy(
+                out=dst.rearrange("p (c i t) -> p c t i", i=4, t=PACK),
+                in_=src.rearrange("p t (c i) -> p c t i", i=4),
+            )
+
+        load_slots = {}
+        load_grouped = {}
+        l_codes = {}
+        l_scales = {}
+
+        flow = {}
+
+        def flow_pass(h, j, t, g):
+            if g == 0:
+                flow[h, j, t] = next_bank([P, HALF])
+            s0 = (g * F_GROUPS + j) * P
+            nc.tensor.matmul_mx(
+                out=flow[h, j, t][:],
+                lhsT=v_codes[g][:, t, 2 * P * j : 2 * P * (j + 1)].bitcast(FP4X4),
+                lhsT_scale=v_scales[:, t, s0 : s0 + P],
+                rhs=a_codes[h, g][:].bitcast(FP8X4),
+                rhs_scale=a_scales[h, g][:],
+                start=(g == 0),
+                stop=(g == K_GROUPS - 1),
+            )
+            if g == K_GROUPS - 1:
+                if t == 0:
+                    load_slots[h, j] = work.tile([P, PACK, HALF], BF16, name="load_slots", tag="load_slots", bufs=3, align_bytes=64)
+                nc.scalar.activation(
+                    out=load_slots[h, j][:, t, :], in_=flow[h, j, t][:], func=ACT.Identity,
+                    scale=inv_service[:, j, t : t + 1], bias=walk_load[:, j, t : t + 1],
+                )
+
+        def flow_slot(h, j, t):
+            for g in range(K_GROUPS):
+                flow_pass(h, j, t, g)
+
+        def interleave_load(h, j, copy):
+            load_grouped[h, j] = work.tile([P, HALF * PACK], BF16, name="load_grouped", tag="load_grouped", align_bytes=64)
+            interleave(load_grouped[h, j][:], load_slots[h, j][:], copy)
+
+        def quantize_load(h, j):
+            l_codes[h, j] = kept("l_codes%d_%d" % (h, j), [P, HALF], U32)
+            l_scales[h, j] = kept("l_scales%d_%d" % (h, j), [P, HALF], U8)
+            quantize(l_codes[h, j][:], l_scales[h, j][:], load_grouped[h, j][:])
+
+        paid = {}
+        y_slots = {}
+        y_grouped = {}
+        y_codes = {}
+        y_scales = [kept("y_scales%d" % h, [P, N_GROUPS, HALF], U8) for h in range(HALVES)]
+
+        def stage2(n):
+            h, G = divmod(n, N_GROUPS)
+            for t in range(PACK):
+                acc = next_bank([P, HALF])
+                for g in range(F_GROUPS):
+                    nc.tensor.matmul_mx(
+                        out=acc[:],
+                        lhsT=r_codes[G][:, t, 2 * P * g : 2 * P * (g + 1)].bitcast(FP4X4),
+                        lhsT_scale=r_scales[G][:, t, P * g : P * (g + 1)],
+                        rhs=l_codes[h, g][:].bitcast(FP8X4),
+                        rhs_scale=l_scales[h, g][:],
+                        start=(g == 0),
+                        stop=(g == F_GROUPS - 1),
+                    )
+                paid[n, t] = work.tile([P, HALF], F32, name="paid", tag="paid", bufs=8, align_bytes=64)
+                nc.scalar.activation(
+                    out=paid[n, t][:], in_=acc[:], func=ACT.Identity,
+                    scale=wage32[:, G, t : t + 1], bias=standing_pay[:, G, t : t + 1],
+                )
+
+        def kink(n, t):
+            G = n % N_GROUPS
+            if t == 0:
+                y_slots[n] = work.tile([P, PACK, HALF], F32, name="y_slots", tag="y_slots", bufs=3, align_bytes=64)
+            nc.vector.scalar_tensor_tensor(
+                out=y_slots[n][:, t, :], in0=paid[n, t][:], scalar=recover32[:, G, t : t + 1], in1=paid[n, t][:],
+                op0=ALU.mult, op1=ALU.max,
+            )
+
+        def interleave_y(n):
+            y_grouped[n] = work.tile([P, HALF * PACK], BF16, name="y_grouped", tag="y_grouped", align_bytes=64)
+            interleave(y_grouped[n][:], y_slots[n][:])
+
+        def quantize_y(n):
+            h, G = divmod(n, N_GROUPS)
+            codes = work.tile([P, HALF], U32, name="y_codes", tag="y_codes", bufs=3, align_bytes=64)
+            quantize(codes[:], y_scales[h][:, G, :], y_grouped[n][:])
+            y_codes[n] = codes
+
+        def store_planes(n):
+            h, G = divmod(n, N_GROUPS)
+            codes = y_codes[n]
+            dst = out_1[G].rearrange("p m t -> p (m t)")[:, PACK * HALF * h : PACK * HALF * (h + 1)]
+            nc.sync.dma_start(out=dst.bitcast(I32), in_=codes[:].bitcast(I32))
+            if G == N_GROUPS - 1:
+                for quad in range(4):
+                    dst = out_2[:, 4 * quad : 4 * quad + 4, HALF * h : HALF * (h + 1)].rearrange("g r m -> r g m")
+                    nc.sync.dma_start(out=dst.bitcast(I32), in_=y_scales[h][32 * quad : 32 * quad + 4].bitcast(I32))
+
+        def turn_y(n, last):
+            h, G = divmod(n, N_GROUPS)
+            rows = work.tile([P, PACK, GROUP], F32, name="y_rows", tag="y_rows", bufs=3, align_bytes=64)
+            for i in range(HALF // P):
+                bank = next_bank([P, PACK, P])
+                for t in range(PACK):
+                    nc.tensor.transpose(bank[:, t, :], y_slots[n][:, t, P * i : P * (i + 1)], ident[:])
+                nc.scalar.copy(out=rows[:, i, :].rearrange("p (r t) -> p r t", t=PACK), in_=bank[:].rearrange("p t r -> p r t"))
+                run = 1 if last else 2
+                if (i + 1) % run == 0:
+                    r0 = HALF * h + P * (i + 1 - run)
+                    dst = out_0[r0 : r0 + run * P, GROUP * G : GROUP * (G + 1)].rearrange("(i p) n -> p i n", p=P)
+                    nc.sync.dma_start(out=dst, in_=rows[:, i + 1 - run : i + 1, :])
+                if last and i == 1:
+                    store_planes(n - 1)
+
+        on_vector = nc.vector.tensor_copy
+        on_scalar = nc.scalar.copy
+        sort_v(0)
+        turn_arrivals(0, 0)
+        sort_v_scales()
+        quantize_arrivals(0, 0)
+        turn_arrivals(0, 1)
+        sort_v(1)
+        for t in range(PACK):
+            flow_pass(0, 0, t, 0)
+        quantize_arrivals(0, 1)
+        turn_arrivals(0, 2)
+        sort_v(2)
+        for t in range(PACK):
+            flow_pass(0, 0, t, 1)
+        nc.vector.reciprocal(out=inv_service[:], in_=service_sb[:])
+        quantize_arrivals(0, 2)
+        nc.vector.tensor_tensor(out=walk_load[:], in0=walk_sb[:], in1=inv_service[:], op=ALU.mult)
+        for t in range(PACK):
+            flow_pass(0, 0, t, 2)
+        sort_r(0)
+        sort_r_scales(0)
+        sort_r(1)
+        for t in range(PACK):
+            flow_slot(0, 1, t)
+        interleave_load(0, 0, on_vector)
+        sort_r_scales(1)
+        quantize_load(0, 0)
+        turn_arrivals(1, 0)
+        turn_arrivals(1, 1)
+        interleave_load(0, 1, on_vector)
+        nc.vector.tensor_tensor(out=standing_pay[:], in0=standing_sb[:], in1=wage_sb[:], op=ALU.mult)
+        quantize_load(0, 1)
+        nc.scalar.copy(out=wage32[:], in_=wage_sb[:])
+        nc.scalar.copy(out=recover32[:], in_=recover_sb[:])
+        turn_arrivals(1, 2)
+        for g in range(K_GROUPS):
+            quantize_arrivals(1, g)
+        units = HALVES * N_GROUPS
+        late_flow = [(j, t) for j in range(F_GROUPS) for t in range(PACK)]
+        for n in range(units):
+            last = n == units - 1
+            stage2(n)
+            kink(n, 0)
+            if n >= 1 and not last:
+                interleave_y(n - 1)
+            kink(n, 1)
+            kink(n, 2)
+            if n >= 1 and not last:
+                quantize_y(n - 1)
+            kink(n, 3)
+            for j, t in late_flow[3 * n : 3 * n + 3]:
+                flow_slot(1, j, t)
+            if n < 2:
+                sort_r(n + 2)
+                sort_r_scales(n + 2)
+            if n >= 1:
+                turn_y(n - 1, False)
+            if n >= 1 and not last:
+                store_planes(n - 1)
+            if n == 1:
+                interleave_load(1, 0, on_vector)
+            if n == 2:
+                interleave_load(1, 1, on_vector)
+                quantize_load(1, 0)
+                quantize_load(1, 1)
+        interleave_y(units - 2)
+        interleave_y(units - 1)
+        quantize_y(units - 2)
+        quantize_y(units - 1)
+        turn_y(units - 1, True)
+        store_planes(units - 1)

@@ -87,10 +87,10 @@ def tile_staffing_wage_swing_h1_kernel(
         load_v(0)
         load_a(0, 0)
         load_scales(v_scale_raw, visit_scales)
-        load_v(1)
         load_a(0, 1)
-        load_v(2)
+        load_v(1)
         load_a(0, 2)
+        load_v(2)
         walk_sb = load_vec("walk_sb", walk_in, F_GROUPS)
         service_sb = load_vec("service_sb", service, F_GROUPS)
         load_r(0)
@@ -112,26 +112,26 @@ def tile_staffing_wage_swing_h1_kernel(
 
         def sort_words(dst, src):
             nc.vector.tensor_copy(
-                out=dst.rearrange("p t (c i b) -> p c t i b", i=LINE // 2, b=2),
-                in_=src.rearrange("p (c i t b) -> p c t i b", i=LINE // 2, t=PACK, b=2),
+                out=dst.rearrange("p t (n b) -> p t n b", b=2),
+                in_=src.rearrange("p (n t b) -> p t n b", t=PACK, b=2),
             )
 
         def sort_v(g):
             sort_words(v_codes[g][:], v_raw[g][:])
 
-        def sort_r(G):
-            sort_words(r_codes[G][:], r_raw[G][:].rearrange("p g b -> p (g b)"))
+        def sort_r(G, t0=0, t1=PACK):
+            nc.vector.tensor_copy(
+                out=r_codes[G][:, t0:t1, :].rearrange("p t (n b) -> p t n b", b=2),
+                in_=r_raw[G][:].rearrange("p g (n t b) -> p t (g n) b", t=PACK, b=2)[:, t0:t1],
+            )
 
         def sort_v_scales():
-            nc.vector.tensor_copy(
-                out=v_scales[:].rearrange("p t (c i) -> p c t i", i=LINE),
-                in_=v_scale_raw[:].rearrange("p g (c i t) -> p (g c) t i", i=LINE, t=PACK),
-            )
+            nc.vector.tensor_copy(out=v_scales[:], in_=v_scale_raw[:].rearrange("p g (n t) -> p t (g n)", t=PACK))
 
         def sort_r_scales(G):
             nc.vector.tensor_copy(
-                out=r_scales[G][:].rearrange("p t (g c i) -> p g c t i", g=F_GROUPS, i=LINE),
-                in_=r_scale_raw[:, :, GROUP * G : GROUP * (G + 1)].rearrange("p g (c i t) -> p g c t i", i=LINE, t=PACK),
+                out=r_scales[G][:].rearrange("p t (g n) -> p t g n", g=F_GROUPS),
+                in_=r_scale_raw[:, :, GROUP * G : GROUP * (G + 1)].rearrange("p g (n t) -> p t g n", t=PACK),
             )
 
         inv_service = kept("inv_service", [P, F_GROUPS, PACK], F32)
@@ -210,34 +210,41 @@ def tile_staffing_wage_swing_h1_kernel(
             l_scales[h, j] = kept("l_scales%d_%d" % (h, j), [P, HALF], U8)
             quantize(l_codes[h, j][:], l_scales[h, j][:], load_grouped[h, j][:])
 
+        unit_of = [divmod(n, N_GROUPS) for n in range(HALVES * N_GROUPS)]
         paid = {}
         y_slots = {}
         y_grouped = {}
         y_codes = {}
         y_scales = [kept("y_scales%d" % h, [P, N_GROUPS, HALF], U8) for h in range(HALVES)]
 
-        def stage2(n):
-            h, G = divmod(n, N_GROUPS)
-            for t in range(PACK):
-                acc = next_bank([P, HALF])
-                for g in range(F_GROUPS):
-                    nc.tensor.matmul_mx(
-                        out=acc[:],
-                        lhsT=r_codes[G][:, t, 2 * P * g : 2 * P * (g + 1)].bitcast(FP4X4),
-                        lhsT_scale=r_scales[G][:, t, P * g : P * (g + 1)],
-                        rhs=l_codes[h, g][:].bitcast(FP8X4),
-                        rhs_scale=l_scales[h, g][:],
-                        start=(g == 0),
-                        stop=(g == F_GROUPS - 1),
-                    )
+        hours = {}
+
+        def hours_pass(n, t, g):
+            h, G = unit_of[n]
+            if g == 0:
+                hours[n, t] = next_bank([P, HALF])
+            nc.tensor.matmul_mx(
+                out=hours[n, t][:],
+                lhsT=r_codes[G][:, t, 2 * P * g : 2 * P * (g + 1)].bitcast(FP4X4),
+                lhsT_scale=r_scales[G][:, t, P * g : P * (g + 1)],
+                rhs=l_codes[h, g][:].bitcast(FP8X4),
+                rhs_scale=l_scales[h, g][:],
+                start=(g == 0),
+                stop=(g == F_GROUPS - 1),
+            )
+            if g == F_GROUPS - 1:
                 paid[n, t] = work.tile([P, HALF], F32, name="paid", tag="paid", bufs=8, align_bytes=64)
                 nc.scalar.activation(
-                    out=paid[n, t][:], in_=acc[:], func=ACT.Identity,
+                    out=paid[n, t][:], in_=hours[n, t][:], func=ACT.Identity,
                     scale=wage32[:, G, t : t + 1], bias=standing_pay[:, G, t : t + 1],
                 )
 
+        def hours_slot(n, t):
+            for g in range(F_GROUPS):
+                hours_pass(n, t, g)
+
         def kink(n, t):
-            G = n % N_GROUPS
+            G = unit_of[n][1]
             if t == 0:
                 y_slots[n] = work.tile([P, PACK, HALF], F32, name="y_slots", tag="y_slots", bufs=3, align_bytes=64)
             nc.vector.scalar_tensor_tensor(
@@ -250,13 +257,13 @@ def tile_staffing_wage_swing_h1_kernel(
             interleave(y_grouped[n][:], y_slots[n][:])
 
         def quantize_y(n):
-            h, G = divmod(n, N_GROUPS)
+            h, G = unit_of[n]
             codes = work.tile([P, HALF], U32, name="y_codes", tag="y_codes", bufs=3, align_bytes=64)
             quantize(codes[:], y_scales[h][:, G, :], y_grouped[n][:])
             y_codes[n] = codes
 
         def store_planes(n):
-            h, G = divmod(n, N_GROUPS)
+            h, G = unit_of[n]
             codes = y_codes[n]
             dst = out_1[G].rearrange("p m t -> p (m t)")[:, PACK * HALF * h : PACK * HALF * (h + 1)]
             nc.sync.dma_start(out=dst.bitcast(I32), in_=codes[:].bitcast(I32))
@@ -265,24 +272,22 @@ def tile_staffing_wage_swing_h1_kernel(
                     dst = out_2[:, 4 * quad : 4 * quad + 4, HALF * h : HALF * (h + 1)].rearrange("g r m -> r g m")
                     nc.sync.dma_start(out=dst.bitcast(I32), in_=y_scales[h][32 * quad : 32 * quad + 4].bitcast(I32))
 
-        def turn_y(n, last):
-            h, G = divmod(n, N_GROUPS)
-            rows = work.tile([P, PACK, GROUP], F32, name="y_rows", tag="y_rows", bufs=3, align_bytes=64)
-            for i in range(HALF // P):
-                bank = next_bank([P, PACK, P])
-                for t in range(PACK):
-                    nc.tensor.transpose(bank[:, t, :], y_slots[n][:, t, P * i : P * (i + 1)], ident[:])
-                nc.scalar.copy(out=rows[:, i, :].rearrange("p (r t) -> p r t", t=PACK), in_=bank[:].rearrange("p t r -> p r t"))
-                run = 1 if last else 2
-                if (i + 1) % run == 0:
-                    r0 = HALF * h + P * (i + 1 - run)
-                    dst = out_0[r0 : r0 + run * P, GROUP * G : GROUP * (G + 1)].rearrange("(i p) n -> p i n", p=P)
-                    nc.sync.dma_start(out=dst, in_=rows[:, i + 1 - run : i + 1, :])
-                if last and i == 1:
-                    store_planes(n - 1)
+        y_rows = {}
+
+        def turn_y(n, i):
+            if i == 0:
+                y_rows[n] = work.tile([P, PACK, GROUP], F32, name="y_rows", tag="y_rows", bufs=3, align_bytes=64)
+            bank = next_bank([P, PACK, P])
+            for t in range(PACK):
+                nc.tensor.transpose(bank[:, t, :], y_slots[n][:, t, P * i : P * (i + 1)], ident[:])
+            nc.scalar.copy(out=y_rows[n][:, i, :].rearrange("p (r t) -> p r t", t=PACK), in_=bank[:].rearrange("p t r -> p r t"))
+
+        def store_rows(n, i0, i1):
+            h, G = unit_of[n]
+            dst = out_0[HALF * h + P * i0 : HALF * h + P * i1, GROUP * G : GROUP * (G + 1)]
+            nc.sync.dma_start(out=dst.rearrange("(i p) n -> p i n", p=P), in_=y_rows[n][:, i0:i1, :])
 
         on_vector = nc.vector.tensor_copy
-        on_scalar = nc.scalar.copy
         sort_v(0)
         turn_arrivals(0, 0)
         sort_v_scales()
@@ -309,47 +314,62 @@ def tile_staffing_wage_swing_h1_kernel(
         interleave_load(0, 0, on_vector)
         sort_r_scales(1)
         quantize_load(0, 0)
-        turn_arrivals(1, 0)
-        turn_arrivals(1, 1)
+        for g in range(2):
+            turn_arrivals(1, g)
+            hours_pass(0, 2 * g, 0)
+            hours_pass(0, 2 * g + 1, 0)
         interleave_load(0, 1, on_vector)
         nc.vector.tensor_tensor(out=standing_pay[:], in0=standing_sb[:], in1=wage_sb[:], op=ALU.mult)
         quantize_load(0, 1)
         nc.scalar.copy(out=wage32[:], in_=wage_sb[:])
         nc.scalar.copy(out=recover32[:], in_=recover_sb[:])
+        hours_pass(0, 0, 1)
+        hours_pass(0, 1, 1)
         turn_arrivals(1, 2)
-        for g in range(K_GROUPS):
-            quantize_arrivals(1, g)
-        units = HALVES * N_GROUPS
-        late_flow = [(j, t) for j in range(F_GROUPS) for t in range(PACK)]
-        for n in range(units):
-            last = n == units - 1
-            stage2(n)
-            kink(n, 0)
-            if n >= 1 and not last:
-                interleave_y(n - 1)
-            kink(n, 1)
-            kink(n, 2)
-            if n >= 1 and not last:
-                quantize_y(n - 1)
-            kink(n, 3)
-            for j, t in late_flow[3 * n : 3 * n + 3]:
-                flow_slot(1, j, t)
-            if n < 2:
-                sort_r(n + 2)
-                sort_r_scales(n + 2)
-            if n >= 1:
-                turn_y(n - 1, False)
-            if n >= 1 and not last:
-                store_planes(n - 1)
-            if n == 1:
-                interleave_load(1, 0, on_vector)
-            if n == 2:
-                interleave_load(1, 1, on_vector)
-                quantize_load(1, 0)
-                quantize_load(1, 1)
-        interleave_y(units - 2)
-        interleave_y(units - 1)
-        quantize_y(units - 2)
-        quantize_y(units - 1)
-        turn_y(units - 1, True)
-        store_planes(units - 1)
+        hours_pass(0, 2, 1)
+        hours_pass(0, 3, 1)
+        quantize_arrivals(1, 0)
+        sort_r(2, 0, 2)
+        quantize_arrivals(1, 1)
+        kink(0, 0)
+        kink(0, 1)
+        sort_r(2, 2, 4)
+        quantize_arrivals(1, 2)
+        kink(0, 2)
+        kink(0, 3)
+        units = len(unit_of)
+        for n in range(1, units):
+            for part in range(2):
+                hours_slot(n, 2 * part)
+                hours_slot(n, 2 * part + 1)
+                if n <= F_GROUPS:
+                    flow_slot(1, n - 1, 2 * part)
+                    flow_slot(1, n - 1, 2 * part + 1)
+                if (n, part) == (1, 0):
+                    sort_r_scales(2)
+                if n in (2, 3) and part == 0:
+                    interleave_load(1, n - 2, on_vector)
+                kink(n, 2 * part)
+                if n in (2, 3) and part == 0:
+                    quantize_load(1, n - 2)
+                kink(n, 2 * part + 1)
+                if part == 0:
+                    interleave_y(n - 1)
+                else:
+                    quantize_y(n - 1)
+                if (n, part) == (1, 0):
+                    sort_r_scales(3)
+                if (n, part) == (1, 1):
+                    sort_r(3)
+                turn_y(n - 1, 2 * part)
+                turn_y(n - 1, 2 * part + 1)
+                store_rows(n - 1, 2 * part, 2 * part + 2)
+            store_planes(n - 1)
+        last = units - 1
+        interleave_y(last)
+        quantize_y(last)
+        for i in range(PACK):
+            turn_y(last, i)
+            if i >= 1:
+                store_rows(last, 0 if i == 1 else i, i + 1)
+        store_planes(last)

@@ -61,7 +61,7 @@ def tile_staffing_wage_swing_h1_kernel(
 
         v_raw = [kept("v_raw%d" % g, [P, 2 * F], U8) for g in range(K_GROUPS)]
         r_raw = [kept("r_raw%d" % G, [P, F_GROUPS, 2 * GROUP], U8) for G in range(N_GROUPS)]
-        a_raw = {(h, g): kept("a_raw%d_%d" % (h, g), [P, HALF // P, GROUP], BF16) for h in range(HALVES) for g in range(K_GROUPS)}
+        a_raw = {(h, g, pair): kept("a_raw%d_%d_%d" % (h, g, pair), [P, 2, GROUP], BF16) for h in range(HALVES) for g in range(K_GROUPS) for pair in range(2)}
 
         def load_v(g):
             nc.sync.dma_start(out=v_raw[g][:].bitcast(I32), in_=visit_words[g].bitcast(I32))
@@ -71,8 +71,10 @@ def tile_staffing_wage_swing_h1_kernel(
             nc.sync.dma_start(out=r_raw[G][:].bitcast(I32), in_=src.bitcast(I32))
 
         def load_a(h, g):
-            src = arrivals[HALF * h : HALF * (h + 1), GROUP * g : GROUP * (g + 1)]
-            nc.sync.dma_start(out=a_raw[h, g][:], in_=src.rearrange("(i p) k -> p i k", p=P))
+            for pair in range(2):
+                m0 = HALF * h + 2 * P * pair
+                src = arrivals[m0 : m0 + 2 * P, GROUP * g : GROUP * (g + 1)]
+                nc.sync.dma_start(out=a_raw[h, g, pair][:], in_=src.rearrange("(i p) k -> p i k", p=P))
 
         def load_scales(raw, dram):
             for quad in range(4):
@@ -106,7 +108,7 @@ def tile_staffing_wage_swing_h1_kernel(
         load_r(3)
 
         v_codes = [kept("v_codes%d" % g, [P, PACK, F // 2], U8) for g in range(K_GROUPS)]
-        v_scales = kept("v_scales", [P, PACK, K_GROUPS * F // PACK], U8)
+        v_scales = [kept("v_scales%d" % g, [P, PACK, F // PACK], U8) for g in range(K_GROUPS)]
         r_codes = [kept("r_codes%d" % G, [P, PACK, F_GROUPS * 2 * P], U8) for G in range(N_GROUPS)]
         r_scales = [kept("r_scales%d" % G, [P, PACK, F_GROUPS * P], U8) for G in range(N_GROUPS)]
 
@@ -125,8 +127,8 @@ def tile_staffing_wage_swing_h1_kernel(
                 in_=r_raw[G][:].rearrange("p g (n t b) -> p t (g n) b", t=PACK, b=2)[:, t0:t1],
             )
 
-        def sort_v_scales():
-            nc.vector.tensor_copy(out=v_scales[:], in_=v_scale_raw[:].rearrange("p g (n t) -> p t (g n)", t=PACK))
+        def sort_v_scales(g):
+            nc.vector.tensor_copy(out=v_scales[g][:], in_=v_scale_raw[:, g, :].rearrange("p (n t) -> p t n", t=PACK))
 
         def sort_r_scales(G):
             nc.vector.tensor_copy(
@@ -144,14 +146,15 @@ def tile_staffing_wage_swing_h1_kernel(
         a_scales = {}
         a_grouped = {}
 
-        def turn_arrivals(h, g):
-            a_grouped[h, g] = work.tile([P, HALF * PACK], BF16, name="a_grouped", tag="a_grouped", bufs=3, align_bytes=64)
-            words = a_raw[h, g][:].bitcast(F32)
-            for pair in range(2):
+        def turn_arrivals(h, g, pairs=(0, 1)):
+            for pair in pairs:
+                if pair == 0:
+                    a_grouped[h, g] = work.tile([P, HALF * PACK], BF16, name="a_grouped", tag="a_grouped", bufs=3, align_bytes=64)
+                words = a_raw[h, g, pair][:].bitcast(F32)
                 bank = next_bank([P, 2, 2 * P])
                 for i in range(2):
                     for u in range(2):
-                        nc.tensor.transpose(bank[:, u, P * i : P * (i + 1)], words[:, 2 * pair + i, u : 2 * P : 2], ident[:])
+                        nc.tensor.transpose(bank[:, u, P * i : P * (i + 1)], words[:, i, u : 2 * P : 2], ident[:])
                 dst = a_grouped[h, g][:].bitcast(F32)[:, 512 * pair : 512 * (pair + 1)]
                 nc.scalar.copy(out=dst.rearrange("p (r u) -> p r u", u=2), in_=bank[:].rearrange("p u r -> p r u"))
 
@@ -179,11 +182,10 @@ def tile_staffing_wage_swing_h1_kernel(
         def flow_pass(h, j, t, g):
             if g == 0:
                 flow[h, j, t] = next_bank([P, HALF])
-            s0 = (g * F_GROUPS + j) * P
             nc.tensor.matmul_mx(
                 out=flow[h, j, t][:],
                 lhsT=v_codes[g][:, t, 2 * P * j : 2 * P * (j + 1)].bitcast(FP4X4),
-                lhsT_scale=v_scales[:, t, s0 : s0 + P],
+                lhsT_scale=v_scales[g][:, t, P * j : P * (j + 1)],
                 rhs=a_codes[h, g][:].bitcast(FP8X4),
                 rhs_scale=a_scales[h, g][:],
                 start=(g == 0),
@@ -290,15 +292,17 @@ def tile_staffing_wage_swing_h1_kernel(
         on_vector = nc.vector.tensor_copy
         sort_v(0)
         turn_arrivals(0, 0)
-        sort_v_scales()
+        sort_v_scales(0)
         quantize_arrivals(0, 0)
         turn_arrivals(0, 1)
-        sort_v(1)
         for t in range(PACK):
             flow_pass(0, 0, t, 0)
-        quantize_arrivals(0, 1)
         turn_arrivals(0, 2)
+        sort_v(1)
+        sort_v_scales(1)
+        quantize_arrivals(0, 1)
         sort_v(2)
+        sort_v_scales(2)
         for t in range(PACK):
             flow_pass(0, 0, t, 1)
         nc.vector.reciprocal(out=inv_service[:], in_=service_sb[:])

from contextlib import ExitStack

import concourse.mybir as mybir
from concourse.masks import make_identity

M, K, F, N = 1024, 1536, 1024, 2048
FLOPS = 2 * M * K * F + 2 * M * F * N

F32 = mybir.dt.float32
BF16 = mybir.dt.bfloat16
I32 = mybir.dt.int32
U32 = mybir.dt.uint32
U8 = mybir.dt.uint8
FP8X4 = mybir.dt.float8_e4m3fn_x4
FP4X4 = mybir.dt.float4_e2m1fn_x4
ALU = mybir.AluOpType
ACT = mybir.ActivationFunctionType

P = 128
PACK = 4
GROUP = P * PACK
HALF = 512
K_GROUPS = K // GROUP
F_GROUPS = F // GROUP
N_GROUPS = N // GROUP
HALVES = M // HALF
LINE = 16


def tile_staffing_wage_swing_h1_kernel(
    tc, arrivals, visit_words, visit_scales, walk_in, service, response_words, response_scales,
    standing, recover, wage, out_0, out_1, out_2,
):
    nc = tc.nc
    with ExitStack() as ctx:
        keep = ctx.enter_context(tc.tile_pool(name="keep", bufs=1))
        work = ctx.enter_context(tc.tile_pool(name="work", bufs=2))
        psum = ctx.enter_context(tc.psum_pool(name="psum", bufs=1))
        ctx.enter_context(tc.manual_schedule())

        def kept(name, shape, dtype):
            return keep.tile(shape, dtype, name=name, align_bytes=64)

        banks_taken = []

        def next_bank(shape):
            name = "bank%d" % (len(banks_taken) % 8)
            banks_taken.append(name)
            return psum.tile(shape, F32, name=name, tag=name)

        ident = kept("ident", [P, P], F32)
        make_identity(nc, ident[:])
        warm_in = kept("warm_in", [P, 1], F32)
        warm_out = kept("warm_out", [P, 1], F32)
        v_scale_raw = kept("v_scale_raw", [P, K_GROUPS, F], U8)
        r_scale_raw = kept("r_scale_raw", [P, F_GROUPS, N], U8)
        nc.vector.memset(v_scale_raw[:].rearrange("p g n -> p (g n)").bitcast(I32), 0)
        nc.vector.memset(warm_in[:], 0.0)
        nc.vector.memset(r_scale_raw[:].rearrange("p g n -> p (g n)").bitcast(I32), 0)
        nc.scalar.activation(out=warm_out[:], in_=warm_in[:], func=ACT.Identity)

        v_raw = [kept("v_raw%d" % g, [P, 2 * F], U8) for g in range(K_GROUPS)]
        r_raw = [kept("r_raw%d" % G, [P, F_GROUPS, 2 * GROUP], U8) for G in range(N_GROUPS)]
        a_raw = {(h, g, pair): kept("a_raw%d_%d_%d" % (h, g, pair), [P, 2, GROUP], BF16) for h in range(HALVES) for g in range(K_GROUPS) for pair in range(2)}

        def load_v(g):
            nc.sync.dma_start(out=v_raw[g][:].bitcast(I32), in_=visit_words[g].bitcast(I32))

        def load_r(G):
            src = response_words[:, :, 2 * GROUP * G : 2 * GROUP * (G + 1)].rearrange("g p b -> p g b")
            nc.sync.dma_start(out=r_raw[G][:].bitcast(I32), in_=src.bitcast(I32))

        def load_a(h, g):
            for pair in range(2):
                m0 = HALF * h + 2 * P * pair
                src = arrivals[m0 : m0 + 2 * P, GROUP * g : GROUP * (g + 1)]
                nc.sync.dma_start(out=a_raw[h, g, pair][:], in_=src.rearrange("(i p) k -> p i k", p=P))

        def load_scales(raw, dram):
            for quad in range(4):
                src = dram[:, 4 * quad : 4 * quad + 4, :].rearrange("g r n -> r g n")
                nc.sync.dma_start(out=raw[32 * quad : 32 * quad + 4].bitcast(I32), in_=src.bitcast(I32))

        def load_vec(name, vec, groups):
            t = kept(name, [P, groups, PACK], BF16)
            nc.sync.dma_start(out=t[:], in_=vec.rearrange("(g p t) -> p g t", p=P, t=PACK))
            return t

        load_v(0)
        load_a(0, 0)
        load_scales(v_scale_raw, visit_scales)
        load_a(0, 1)
        load_v(1)
        load_a(0, 2)
        load_v(2)
        walk_sb = load_vec("walk_sb", walk_in, F_GROUPS)
        service_sb = load_vec("service_sb", service, F_GROUPS)
        load_r(0)
        load_scales(r_scale_raw, response_scales)
        load_r(1)
        load_a(1, 0)
        load_a(1, 1)
        load_a(1, 2)
        standing_sb = load_vec("standing_sb", standing, N_GROUPS)
        recover_sb = load_vec("recover_sb", recover, N_GROUPS)
        wage_sb = load_vec("wage_sb", wage, N_GROUPS)
        load_r(2)
        load_r(3)

        v_codes = [kept("v_codes%d" % g, [P, PACK, F // 2], U8) for g in range(K_GROUPS)]
        v_scales = [kept("v_scales%d" % g, [P, PACK, F // PACK], U8) for g in range(K_GROUPS)]
        r_codes = [kept("r_codes%d" % G, [P, PACK, F_GROUPS * 2 * P], U8) for G in range(N_GROUPS)]
        r_scales = [kept("r_scales%d" % G, [P, PACK, F_GROUPS * P], U8) for G in range(N_GROUPS)]

        def sort_words(dst, src):
            nc.vector.tensor_copy(
                out=dst.rearrange("p t (n b) -> p t n b", b=2),
                in_=src.rearrange("p (n t b) -> p t n b", t=PACK, b=2),
            )

        def sort_v(g):
            sort_words(v_codes[g][:], v_raw[g][:])

        def sort_r(G, t0=0, t1=PACK):
            nc.vector.tensor_copy(
                out=r_codes[G][:, t0:t1, :].rearrange("p t (n b) -> p t n b", b=2),
                in_=r_raw[G][:].rearrange("p g (n t b) -> p t (g n) b", t=PACK, b=2)[:, t0:t1],
            )

        def sort_v_scales(g):
            nc.vector.tensor_copy(out=v_scales[g][:], in_=v_scale_raw[:, g, :].rearrange("p (n t) -> p t n", t=PACK))

        def sort_r_scales(G):
            nc.vector.tensor_copy(
                out=r_scales[G][:].rearrange("p t (g n) -> p t g n", g=F_GROUPS),
                in_=r_scale_raw[:, :, GROUP * G : GROUP * (G + 1)].rearrange("p g (n t) -> p t g n", t=PACK),
            )

        inv_service = kept("inv_service", [P, F_GROUPS, PACK], F32)
        walk_load = kept("walk_load", [P, F_GROUPS, PACK], F32)
        wage32 = kept("wage32", [P, N_GROUPS, PACK], F32)
        recover32 = kept("recover32", [P, N_GROUPS, PACK], F32)
        standing_pay = kept("standing_pay", [P, N_GROUPS, PACK], F32)

        a_codes = {}
        a_scales = {}
        a_grouped = {}

        def turn_arrivals(h, g, pairs=(0, 1)):
            for pair in pairs:
                if pair == 0:
                    a_grouped[h, g] = work.tile([P, HALF * PACK], BF16, name="a_grouped", tag="a_grouped", bufs=3, align_bytes=64)
                words = a_raw[h, g, pair][:].bitcast(F32)
                bank = next_bank([P, 2, 2 * P])
                for i in range(2):
                    for u in range(2):
                        nc.tensor.transpose(bank[:, u, P * i : P * (i + 1)], words[:, i, u : 2 * P : 2], ident[:])
                dst = a_grouped[h, g][:].bitcast(F32)[:, 512 * pair : 512 * (pair + 1)]
                nc.scalar.copy(out=dst.rearrange("p (r u) -> p r u", u=2), in_=bank[:].rearrange("p u r -> p r u"))

        def quantize(codes, scales, grouped):
            nc.vector.quantize_mx(out=codes.bitcast(FP8X4), scales=scales, in_=grouped)

        def quantize_arrivals(h, g):
            a_codes[h, g] = kept("a_codes%d_%d" % (h, g), [P, HALF], U32)
            a_scales[h, g] = kept("a_scales%d_%d" % (h, g), [P, HALF], U8)
            quantize(a_codes[h, g][:], a_scales[h, g][:], a_grouped[h, g][:])

        def interleave(dst, src, copy=nc.vector.tensor_copy):
            copy(
                out=dst.rearrange("p (c i t) -> p c t i", i=4, t=PACK),
                in_=src.rearrange("p t (c i) -> p c t i", i=4),
            )

        load_slots = {}
        load_grouped = {}
        l_codes = {}
        l_scales = {}

        flow = {}

        def flow_pass(h, j, t, g):
            if g == 0:
                flow[h, j, t] = next_bank([P, HALF])
            nc.tensor.matmul_mx(
                out=flow[h, j, t][:],
                lhsT=v_codes[g][:, t, 2 * P * j : 2 * P * (j + 1)].bitcast(FP4X4),
                lhsT_scale=v_scales[g][:, t, P * j : P * (j + 1)],
                rhs=a_codes[h, g][:].bitcast(FP8X4),
                rhs_scale=a_scales[h, g][:],
                start=(g == 0),
                stop=(g == K_GROUPS - 1),
            )
            if g == K_GROUPS - 1:
                if t == 0:
                    load_slots[h, j] = work.tile([P, PACK, HALF], BF16, name="load_slots", tag="load_slots", bufs=3, align_bytes=64)
                nc.scalar.activation(
                    out=load_slots[h, j][:, t, :], in_=flow[h, j, t][:], func=ACT.Identity,
                    scale=inv_service[:, j, t : t + 1], bias=walk_load[:, j, t : t + 1],
                )

        def flow_slot(h, j, t):
            for g in range(K_GROUPS):
                flow_pass(h, j, t, g)

        def interleave_load(h, j, copy):
            load_grouped[h, j] = work.tile([P, HALF * PACK], BF16, name="load_grouped", tag="load_grouped", align_bytes=64)
            interleave(load_grouped[h, j][:], load_slots[h, j][:], copy)

        def quantize_load(h, j):
            l_codes[h, j] = kept("l_codes%d_%d" % (h, j), [P, HALF], U32)
            l_scales[h, j] = kept("l_scales%d_%d" % (h, j), [P, HALF], U8)
            quantize(l_codes[h, j][:], l_scales[h, j][:], load_grouped[h, j][:])

        unit_of = [divmod(n, N_GROUPS) for n in range(HALVES * N_GROUPS)]
        paid = {}
        y_slots = {}
        y_grouped = {}
        y_codes = {}
        y_scales = [kept("y_scales%d" % h, [P, N_GROUPS, HALF], U8) for h in range(HALVES)]

        hours = {}

        def hours_pass(n, t, g):
            h, G = unit_of[n]
            if g == 0:
                hours[n, t] = next_bank([P, HALF])
            nc.tensor.matmul_mx(
                out=hours[n, t][:],
                lhsT=r_codes[G][:, t, 2 * P * g : 2 * P * (g + 1)].bitcast(FP4X4),
                lhsT_scale=r_scales[G][:, t, P * g : P * (g + 1)],
                rhs=l_codes[h, g][:].bitcast(FP8X4),
                rhs_scale=l_scales[h, g][:],
                start=(g == 0),
                stop=(g == F_GROUPS - 1),
            )
            if g == F_GROUPS - 1:
                paid[n, t] = work.tile([P, HALF], F32, name="paid", tag="paid", bufs=8, align_bytes=64)
                nc.scalar.activation(
                    out=paid[n, t][:], in_=hours[n, t][:], func=ACT.Identity,
                    scale=wage32[:, G, t : t + 1], bias=standing_pay[:, G, t : t + 1],
                )

        def hours_slot(n, t):
            for g in range(F_GROUPS):
                hours_pass(n, t, g)

        def kink(n, t):
            G = unit_of[n][1]
            if t == 0:
                y_slots[n] = work.tile([P, PACK, HALF], F32, name="y_slots", tag="y_slots", bufs=3, align_bytes=64)
            nc.vector.scalar_tensor_tensor(
                out=y_slots[n][:, t, :], in0=paid[n, t][:], scalar=recover32[:, G, t : t + 1], in1=paid[n, t][:],
                op0=ALU.mult, op1=ALU.max,
            )

        def interleave_y(n):
            y_grouped[n] = work.tile([P, HALF * PACK], BF16, name="y_grouped", tag="y_grouped", align_bytes=64)
            interleave(y_grouped[n][:], y_slots[n][:])

        def quantize_y(n):
            h, G = unit_of[n]
            codes = work.tile([P, HALF], U32, name="y_codes", tag="y_codes", bufs=3, align_bytes=64)
            quantize(codes[:], y_scales[h][:, G, :], y_grouped[n][:])
            y_codes[n] = codes

        def store_planes(n):
            h, G = unit_of[n]
            codes = y_codes[n]
            dst = out_1[G].rearrange("p m t -> p (m t)")[:, PACK * HALF * h : PACK * HALF * (h + 1)]
            nc.sync.dma_start(out=dst.bitcast(I32), in_=codes[:].bitcast(I32))
            if G == N_GROUPS - 1:
                for quad in range(4):
                    dst = out_2[:, 4 * quad : 4 * quad + 4, HALF * h : HALF * (h + 1)].rearrange("g r m -> r g m")
                    nc.sync.dma_start(out=dst.bitcast(I32), in_=y_scales[h][32 * quad : 32 * quad + 4].bitcast(I32))

        y_rows = {}

        def turn_y(n, i):
            if i == 0:
                y_rows[n] = work.tile([P, PACK, GROUP], F32, name="y_rows", tag="y_rows", bufs=3, align_bytes=64)
            bank = next_bank([P, PACK, P])
            for t in range(PACK):
                nc.tensor.transpose(bank[:, t, :], y_slots[n][:, t, P * i : P * (i + 1)], ident[:])
            nc.scalar.copy(out=y_rows[n][:, i, :].rearrange("p (r t) -> p r t", t=PACK), in_=bank[:].rearrange("p t r -> p r t"))

        def store_rows(n, i0, i1):
            h, G = unit_of[n]
            dst = out_0[HALF * h + P * i0 : HALF * h + P * i1, GROUP * G : GROUP * (G + 1)]
            nc.sync.dma_start(out=dst.rearrange("(i p) n -> p i n", p=P), in_=y_rows[n][:, i0:i1, :])

        on_vector = nc.vector.tensor_copy
        sort_v(0)
        turn_arrivals(0, 0)
        sort_v_scales(0)
        quantize_arrivals(0, 0)
        turn_arrivals(0, 1)
        for t in range(PACK):
            flow_pass(0, 0, t, 0)
        turn_arrivals(0, 2)
        sort_v(1)
        sort_v_scales(1)
        quantize_arrivals(0, 1)
        sort_v(2)
        sort_v_scales(2)
        for t in range(PACK):
            flow_pass(0, 0, t, 1)
        nc.vector.reciprocal(out=inv_service[:], in_=service_sb[:])
        quantize_arrivals(0, 2)
        nc.vector.tensor_tensor(out=walk_load[:], in0=walk_sb[:], in1=inv_service[:], op=ALU.mult)
        for t in range(PACK):
            flow_pass(0, 0, t, 2)
        sort_r(0)
        sort_r_scales(0)
        sort_r(1)
        for t in range(PACK):
            flow_slot(0, 1, t)
        interleave_load(0, 0, on_vector)
        sort_r_scales(1)
        quantize_load(0, 0)
        for g in range(2):
            turn_arrivals(1, g)
            hours_pass(0, 2 * g, 0)
            hours_pass(0, 2 * g + 1, 0)
        interleave_load(0, 1, on_vector)
        nc.vector.tensor_tensor(out=standing_pay[:], in0=standing_sb[:], in1=wage_sb[:], op=ALU.mult)
        quantize_load(0, 1)
        nc.scalar.copy(out=wage32[:], in_=wage_sb[:])
        nc.scalar.copy(out=recover32[:], in_=recover_sb[:])
        hours_pass(0, 0, 1)
        hours_pass(0, 1, 1)
        turn_arrivals(1, 2)
        hours_pass(0, 2, 1)
        hours_pass(0, 3, 1)
        quantize_arrivals(1, 0)
        sort_r(2, 0, 2)
        quantize_arrivals(1, 1)
        kink(0, 0)
        kink(0, 1)
        sort_r(2, 2, 4)
        quantize_arrivals(1, 2)
        kink(0, 2)
        kink(0, 3)
        units = len(unit_of)
        for n in range(1, units):
            for part in range(2):
                hours_slot(n, 2 * part)
                hours_slot(n, 2 * part + 1)
                if n <= F_GROUPS:
                    flow_slot(1, n - 1, 2 * part)
                    flow_slot(1, n - 1, 2 * part + 1)
                if (n, part) == (1, 0):
                    sort_r_scales(2)
                if n in (2, 3) and part == 0:
                    interleave_load(1, n - 2, on_vector)
                kink(n, 2 * part)
                if n in (2, 3) and part == 0:
                    quantize_load(1, n - 2)
                kink(n, 2 * part + 1)
                if part == 0:
                    interleave_y(n - 1)
                else:
                    quantize_y(n - 1)
                if (n, part) == (1, 0):
                    sort_r_scales(3)
                if (n, part) == (1, 1):
                    sort_r(3)
                turn_y(n - 1, 2 * part)
                turn_y(n - 1, 2 * part + 1)
                store_rows(n - 1, 2 * part, 2 * part + 2)
            store_planes(n - 1)
        last = units - 1
        interleave_y(last)
        quantize_y(last)
        for i in range(PACK):
            turn_y(last, i)
            if i >= 1:
                store_rows(last, 0 if i == 1 else i, i + 1)
        store_planes(last)
